import numpy as np
import ml_dtypes


def mxq(x, axis, fmt="e4m3"):
    dtype, down = {"e4m3": (ml_dtypes.float8_e4m3fn, 7), "e5m2": (ml_dtypes.float8_e5m2, 14)}[fmt]
    v = np.moveaxis(np.asarray(x, np.float32).astype(ml_dtypes.bfloat16).astype(np.float64), axis, -1)
    blocks = v.reshape(v.shape[:-1] + (-1, 32))
    amax = np.abs(blocks).max(-1, keepdims=True)
    byte = np.maximum(np.where(amax > 0, np.frexp(amax)[1] - 1 + 127, 0) - down, 1)
    scale = np.exp2(byte - 127.0)
    codes = (blocks / scale).astype(np.float32).astype(dtype).astype(np.float64)
    return np.moveaxis((codes * scale).reshape(v.shape), -1, axis)


WIDE = False


def mx_kscale(k):
    if not WIDE:
        return np.ones(k)
    levels = np.array([24, -24, 12, -12, 0])
    if k % 512:
        return np.exp2(np.random.permutation(np.resize(levels, k // 32))).repeat(32)
    a = np.empty((k // 512, 16))
    for p in range(k // 512):
        a[p, :8] = np.random.permutation(np.resize(levels, 8))
        for g in range(8):
            far = levels[np.abs(levels - a[p, g]) >= 10]
            a[p, g + 8] = far[np.random.randint(len(far))]
    return np.exp2(a.ravel()).repeat(32)


def f64(x):
    return np.asarray(x).astype(np.float64)


def striped(idx):
    return np.tile(idx.reshape(-1, 16).T, (8, 1)).astype(np.uint16)


def unstriped(offs):
    return offs[:16].T.reshape(-1).astype(np.int64)


E2M1 = np.array([0.0, 0.5, 1.0, 1.5, 2.0, 3.0, 4.0, 6.0, -0.0, -0.5, -1.0, -1.5, -2.0, -3.0, -4.0, -6.0])


def pack_weight(w, fmt):
    k, n = w.shape
    w = f64(np.asarray(w, np.float32).astype(ml_dtypes.bfloat16)).reshape(k // 32, 32, n)
    amax = np.abs(w).max(1)
    if fmt == "e4m3":
        byte = np.frexp(amax)[1] - 1 + 127 - 7
    else:
        mant, ex = np.frexp(amax / 6.0)
        byte = np.where(mant > 0.5, ex, ex - 1) + 127
    byte = np.clip(np.where(amax > 0, byte, 1), 1, 254)
    scaled = (w * np.exp2(127.0 - byte)[:, None, :]).reshape(k, n).astype(np.float32)
    by_word = np.ascontiguousarray(scaled.reshape(k // 512, 128, 4, n).transpose(0, 1, 3, 2))
    if fmt == "e4m3":
        words = by_word.astype(ml_dtypes.float8_e4m3fn).view(np.uint8)
    else:
        c = by_word.astype(ml_dtypes.float4_e2m1fn).view(np.uint8) & 0xF
        words = (c[..., 0::2] | (c[..., 1::2] << 4)).reshape(k // 512, 128, 2 * n)
    return np.ascontiguousarray(words), np.ascontiguousarray(byte.astype(np.uint8).reshape(k // 512, 16, n))


def unpack_weight(words, scales, fmt):
    g, _, n = scales.shape
    words = np.ascontiguousarray(words).reshape(g, 128, n, -1)
    if fmt == "e4m3":
        vals = words.view(ml_dtypes.float8_e4m3fn).astype(np.float64)
    else:
        nib = np.empty((g, 128, n, 4), np.uint8)
        nib[..., 0::2] = words & 0xF
        nib[..., 1::2] = words >> 4
        vals = E2M1[nib]
    vals = vals * np.repeat(np.exp2(scales.astype(np.float64) - 127.0), 8, axis=1)[..., None]
    return vals.transpose(0, 1, 3, 2).reshape(g * 512, n)


def pack_table4(v):
    words, scales = pack_weight(v, "e2m1")
    g, t = words.shape[0] // 2, v.shape[1]
    return np.ascontiguousarray(words.reshape(g, 2, 128, t, 2).transpose(0, 2, 3, 1, 4).reshape(g, 128, t, 4)), scales


def unpack_table4(words, scales):
    g, _, t, _ = words.shape
    return unpack_weight(words.reshape(g, 128, t, 2, 2).transpose(0, 3, 1, 2, 4).reshape(2 * g, 128, 2 * t), scales, "e2m1")


def silu(f):
    return f / (1.0 + np.exp(-np.maximum(f, -700.0)))


K, M, N, J, T = 1024, 512, 256, 2048, 4096


def setup_inputs():
    n = np.random.standard_normal
    s = mx_kscale(K)[:, None]
    u = mx_kscale(J)[:, None]
    p_tab = pack_table4(0.5 * n((K, T)) / np.sqrt(K) / s)
    p_al = pack_weight(n((J, N)) / np.sqrt(J) / u, "e4m3")
    return {
        "x": (n((K, M)) * s).astype(np.float32),
        "tab_words": p_tab[0],
        "tab_scales": p_tab[1],
        "cw": (np.random.uniform(0.5, 2.0, J) * u[:, 0]).astype(np.float32),
        "cb": (0.3 * n(J)).astype(np.float32),
        "al_words": p_al[0],
        "al_scales": p_al[1],
        "b": (0.3 * n(N)).astype(np.float32),
        "offs": striped(np.random.permutation(T)[:J]),
    }


def reference(x, tab_words, tab_scales, cw, cb, al_words, al_scales, b, offs):
    idx = unstriped(offs)
    x_ = mxq(f64(x), 0, "e4m3")
    tab_ = unpack_table4(tab_words, tab_scales)[:, idx]
    d = tab_.T @ x_
    h = f64(cw)[:, None] * (d + f64(cb)[:, None]) ** 2
    h_ = mxq(h, 0, "e4m3")
    al_ = unpack_weight(al_words, al_scales, "e4m3")
    y = al_.T @ h_
    return silu(y + f64(b)[:, None])

@@ -1,0 +1,216 @@
+from contextlib import ExitStack
+
+import concourse.mybir as mybir
+
+K, M, N, J, T = 1024, 512, 256, 2048, 4096
+FLOPS = 2 * K * M * J + 2 * J * M * N
+
+F32 = mybir.dt.float32
+BF16 = mybir.dt.bfloat16
+I32 = mybir.dt.int32
+U32 = mybir.dt.uint32
+U16 = mybir.dt.uint16
+U8 = mybir.dt.uint8
+FP8X4 = mybir.dt.float8_e4m3fn_x4
+FP4X4 = mybir.dt.float4_e2m1fn_x4
+ACT = mybir.ActivationFunctionType
+ALU = mybir.AluOpType
+
+P = 128
+PACK = 4
+PASS = P * PACK
+K_PASSES = K // PASS
+J_PASSES = J // PASS
+N_TILES = N // P
+QUADS = 4
+X_HALF = M // 2
+SQRT_FLOOR = 2.0 ** -116
+
+
+def interleave(copy, dst, src):
+    copy(
+        out=dst.rearrange("p (c i) t -> p c t i", i=PACK),
+        in_=src.rearrange("p t (c i) -> p c t i", i=PACK),
+    )
+
+
+def tile_list_kernl_poly2_silu_kernel(
+    tc, x, tab_words, tab_scales, cw, cb, al_words, al_scales, b, offs, out
+):
+    nc = tc.nc
+    with ExitStack() as ctx:
+        keep = ctx.enter_context(tc.tile_pool(name="keep", bufs=1))
+        ring = ctx.enter_context(tc.tile_pool(name="ring", bufs=2))
+        psum_d = ctx.enter_context(tc.psum_pool(name="psum_d", bufs=6))
+        psum_y = ctx.enter_context(tc.psum_pool(name="psum_y", bufs=1))
+
+        offsets = keep.tile([P, J // 16], U16, name="offsets")
+        nc.sync.dma_start(offsets[:], offs)
+
+        scale_win = keep.tile([P, T], U8, name="scale_win", align_bytes=64)
+        nc.sync.dma_start(
+            scale_win[0:32, :].bitcast(I32),
+            tab_scales.rearrange("a q t -> (a q) t").bitcast(I32),
+        )
+        nc.gpsimd.memset(scale_win[32:64, :].bitcast(I32), 0)
+        nc.gpsimd.memset(scale_win[64:128, :].bitcast(I32), 0)
+
+        x_raw = {}
+
+        def load_x(a):
+            for h in range(2):
+                x_raw[a, h] = keep.tile([P, PACK, X_HALF], F32, name=f"x_raw{a}{h}")
+                nc.sync.dma_start(
+                    x_raw[a, h][:],
+                    x[a * PASS : (a + 1) * PASS, h * X_HALF : (h + 1) * X_HALF].rearrange("(p t) m -> p t m", t=PACK),
+                )
+
+        load_x(0)
+
+        word_win = keep.tile([P, T], U32, name="word_win", align_bytes=64)
+        nc.sync.dma_start(
+            word_win[:].bitcast(I32),
+            tab_words[0].rearrange("p t i -> p (t i)").bitcast(I32),
+        )
+
+        cw_sb = keep.tile([P, J_PASSES, PACK], F32, name="cw_sb")
+        cb_sb = keep.tile([P, J_PASSES, PACK], F32, name="cb_sb")
+        nc.scalar.dma_start(cw_sb[:], cw.rearrange("(g p t) -> p g t", g=J_PASSES, t=PACK))
+        nc.scalar.dma_start(cb_sb[:], cb.rearrange("(g p t) -> p g t", g=J_PASSES, t=PACK))
+
+        load_x(1)
+
+        plane1 = keep.tile([P, J], U8, name="plane1", align_bytes=64)
+        nc.vector.memset(plane1[:].bitcast(I32), 0)
+
+        cw_flat = cw_sb[:].rearrange("p g t -> p (g t)")
+        cb_flat = cb_sb[:].rearrange("p g t -> p (g t)")
+        sign = keep.tile([P, J_PASSES * PACK], F32, name="sign")
+        mag = keep.tile([P, J_PASSES * PACK], F32, name="mag")
+        root = keep.tile([P, J_PASSES * PACK], F32, name="root")
+        shift = keep.tile([P, J_PASSES * PACK], F32, name="shift")
+        nc.scalar.activation(sign[:], cw_flat, ACT.Sign)
+        nc.scalar.activation(mag[:], cw_flat, ACT.Abs)
+        nc.scalar.activation(root[:], mag[:], ACT.Sqrt, bias=SQRT_FLOOR)
+
+        scale_picked = keep.tile([P, J], U8, name="scale_picked", tag="scale_picked", align_bytes=64)
+        nc.vector.tensor_copy(scale_picked[:], scale_win[:].indirect(offsets[:]))
+        plane0 = keep.tile([P, J], U8, name="plane0", align_bytes=64)
+        nc.vector.tensor_copy(
+            out=plane0[:].rearrange("q (g t p) -> q g p t", g=J_PASSES, t=PACK),
+            in_=scale_picked[:].rearrange("q (g p t) -> q g p t", g=J_PASSES, t=PACK),
+        )
+        for q in range(1, QUADS):
+            nc.sync.dma_start(plane0[32 * q : 32 * q + 4, :].bitcast(I32), plane0[4 * q : 4 * q + 4, :].bitcast(I32))
+        for q in range(QUADS):
+            nc.sync.dma_start(
+                plane1[32 * q : 32 * q + 4, :].bitcast(I32), plane0[16 + 4 * q : 20 + 4 * q, :].bitcast(I32)
+            )
+        planes = (plane0, plane1)
+
+        nc.vector.tensor_tensor(shift[:], root[:], cb_flat, ALU.mult)
+
+
+        centres = {}
+
+        def pick_words(g):
+            picked = keep.tile([P, PASS], U32, name="picked", align_bytes=64)
+            nc.vector.tensor_copy(picked[:], word_win[:].indirect(offsets[:, 32 * g : 32 * (g + 1)]))
+            return picked
+
+        def part_words(g, picked):
+            centres[g] = keep.tile([P, K_PASSES * PASS * 2], U8, name=f"centres{g}", tag="x_woven1" if g == 2 else f"centres{g}", align_bytes=64)
+            nc.vector.tensor_copy(
+                out=centres[g][:].bitcast(U16).rearrange("q (d t p) -> q d p t", d=K_PASSES, t=PACK),
+                in_=picked[:].bitcast(U16).rearrange("q (p t d) -> q d p t", d=K_PASSES, t=PACK),
+            )
+
+        x_codes = [keep.tile([P, M], U32, name=f"x_codes{a}", align_bytes=64) for a in range(K_PASSES)]
+        x_planes = [keep.tile([P, M], U8, name=f"x_plane{a}", align_bytes=64) for a in range(K_PASSES)]
+
+        def quantize_x(a):
+            woven = keep.tile([P, M, PACK], BF16, name=f"x_woven{a}", tag=f"x_woven{a}", align_bytes=64)
+            for h in range(2):
+                interleave(nc.scalar.copy, woven[:, h * X_HALF : (h + 1) * X_HALF, :], x_raw[a, h][:])
+            nc.vector.quantize_mx(
+                out=x_codes[a][:].bitcast(FP8X4),
+                scales=x_planes[a][:],
+                in_=woven[:].rearrange("p m t -> p (m t)"),
+            )
+
+        y_acc = [psum_y.tile([P, M], F32, name=f"y_acc{c}") for c in range(N_TILES)]
+
+        def first_stage(g):
+            h_rows = ring.tile([P, PACK, M], BF16, name="h_rows", align_bytes=64)
+            for t in range(PACK):
+                d_acc = psum_d.tile([P, M], F32, name="d_acc")
+                for a in range(K_PASSES):
+                    col = (a * PACK + t) * P
+                    nc.tensor.matmul_mx(
+                        out=d_acc[:],
+                        lhsT=centres[g][:, 2 * col : 2 * (col + P)].bitcast(FP4X4),
+                        lhsT_scale=planes[a][:, g * PASS + t * P : g * PASS + (t + 1) * P],
+                        rhs=x_codes[a][:].bitcast(FP8X4),
+                        rhs_scale=x_planes[a][:],
+                        start=(a == 0),
+                        stop=(a == K_PASSES - 1),
+                    )
+                u = g * PACK + t
+                nc.scalar.activation(
+                    h_rows[:, t, :], d_acc[:], ACT.Square, bias=shift[:, u : u + 1], scale=root[:, u : u + 1]
+                )
+                nc.vector.tensor_scalar(h_rows[:, t, :], h_rows[:, t, :], sign[:, u : u + 1], None, ALU.mult)
+            return h_rows
+
+        def second_stage(g, h_rows):
+            woven = ring.tile([P, M, PACK], BF16, name="h_woven", align_bytes=64)
+            interleave(nc.vector.tensor_copy, woven[:], h_rows[:])
+            h_codes = ring.tile([P, M], U32, name="h_codes", align_bytes=64)
+            h_plane = ring.tile([P, M], U8, name="h_plane", align_bytes=64)
+            nc.vector.quantize_mx(
+                out=h_codes[:].bitcast(FP8X4),
+                scales=h_plane[:],
+                in_=woven[:].rearrange("p m t -> p (m t)"),
+            )
+            for c in range(N_TILES):
+                nc.tensor.matmul_mx(
+                    out=y_acc[c][:],
+                    lhsT=al_codes[:, g, c * P : (c + 1) * P].bitcast(FP8X4),
+                    lhsT_scale=al_plane[4 * g :, c * P : (c + 1) * P],
+                    rhs=h_codes[:].bitcast(FP8X4),
+                    rhs_scale=h_plane[:],
+                    start=(g == 0),
+                    stop=(g == J_PASSES - 1),
+                )
+
+        quantize_x(0)
+        al_codes = keep.tile([P, J_PASSES, N], U32, name="al_codes", tag="x_woven0", align_bytes=64)
+        nc.sync.dma_start(
+            al_codes[:].bitcast(I32),
+            al_words.rearrange("g p n i -> p g (n i)").bitcast(I32),
+        )
+        al_plane = keep.tile([P, N], U8, name="al_plane", tag="scale_picked", align_bytes=64)
+        nc.gpsimd.memset(al_plane[:].bitcast(I32), 0)
+        for q in range(QUADS):
+            nc.sync.dma_start(
+                al_plane[32 * q : 32 * q + 16, :].bitcast(I32),
+                al_scales[:, 4 * q : 4 * q + 4, :].bitcast(I32),
+            )
+        b_sb = keep.tile([P, N_TILES], F32, name="b_sb")
+        with nc.allow_non_contiguous_dma(reason="one bias value a partition"):
+            nc.sync.dma_start(b_sb[:], b.rearrange("(c p) -> p c", p=P))
+
+        for g in range(J_PASSES):
+            if g == 2:
+                quantize_x(1)
+            part_words(g, pick_words(g))
+        rows = first_stage(0)
+        for g in range(J_PASSES):
+            nxt = first_stage(g + 1) if g + 1 < J_PASSES else None
+            second_stage(g, rows)
+            rows = nxt
+
+        for c in range(N_TILES):
+            result = keep.tile([P, M], F32, name=f"result{c}")
+            nc.scalar.activation(result[:], y_acc[c][:], ACT.Silu, bias=b_sb[:, c : c + 1])
+            nc.sync.dma_start(out[c * P : (c + 1) * P, :], result[:])

@@ -1,6 +1,7 @@
 from contextlib import ExitStack
 
 import concourse.mybir as mybir
+from concourse.masks import make_identity
 
 K, M, N, J, T = 1024, 512, 256, 2048, 4096
 FLOPS = 2 * K * M * J + 2 * J * M * N
@@ -23,8 +24,11 @@ K_PASSES = K // PASS
 J_PASSES = J // PASS
 N_TILES = N // P
 QUADS = 4
-X_HALF = M // 2
+HALF = M // 2
+CW_ROW = P - 2 * J_PASSES
+CB_ROW = P - J_PASSES
 SQRT_FLOOR = 2.0 ** -116
+LAST = J_PASSES - 1
 
 
 def interleave(copy, dst, src):
@@ -41,8 +45,7 @@ def tile_list_kernl_poly2_silu_kernel(
     with ExitStack() as ctx:
         keep = ctx.enter_context(tc.tile_pool(name="keep", bufs=1))
         ring = ctx.enter_context(tc.tile_pool(name="ring", bufs=2))
-        psum_d = ctx.enter_context(tc.psum_pool(name="psum_d", bufs=6))
-        psum_y = ctx.enter_context(tc.psum_pool(name="psum_y", bufs=1))
+        psum = ctx.enter_context(tc.psum_pool(name="psum", bufs=8))
 
         offsets = keep.tile([P, J // 16], U16, name="offsets")
         nc.sync.dma_start(offsets[:], offs)
@@ -52,20 +55,16 @@ def tile_list_kernl_poly2_silu_kernel(
             scale_win[0:32, :].bitcast(I32),
             tab_scales.rearrange("a q t -> (a q) t").bitcast(I32),
         )
-        nc.gpsimd.memset(scale_win[32:64, :].bitcast(I32), 0)
-        nc.gpsimd.memset(scale_win[64:128, :].bitcast(I32), 0)
+        nc.vector.memset(scale_win[32:64, :].bitcast(I32), 0)
+        nc.vector.memset(scale_win[64:128, :].bitcast(I32), 0)
 
-        x_raw = {}
+        rows = keep.tile([P, PASS], F32, name="rows", tag="rows", align_bytes=64)
+        nc.gpsimd.memset(rows[0:CW_ROW, :], 0.0)
+        nc.sync.dma_start(rows[CW_ROW:CB_ROW, :], cw.rearrange("(g j) -> g j", g=J_PASSES))
+        nc.sync.dma_start(rows[CB_ROW:P, :], cb.rearrange("(g j) -> g j", g=J_PASSES))
 
-        def load_x(a):
-            for h in range(2):
-                x_raw[a, h] = keep.tile([P, PACK, X_HALF], F32, name=f"x_raw{a}{h}")
-                nc.sync.dma_start(
-                    x_raw[a, h][:],
-                    x[a * PASS : (a + 1) * PASS, h * X_HALF : (h + 1) * X_HALF].rearrange("(p t) m -> p t m", t=PACK),
-                )
-
-        load_x(0)
+        x_first = keep.tile([P, PACK, M], F32, name="x_first", tag="x_first", align_bytes=64)
+        nc.sync.dma_start(x_first[:], x[0:PASS, :].rearrange("(p t) m -> p t m", t=PACK))
 
         word_win = keep.tile([P, T], U32, name="word_win", align_bytes=64)
         nc.sync.dma_start(
@@ -73,144 +72,204 @@ def tile_list_kernl_poly2_silu_kernel(
             tab_words[0].rearrange("p t i -> p (t i)").bitcast(I32),
         )
 
-        cw_sb = keep.tile([P, J_PASSES, PACK], F32, name="cw_sb")
-        cb_sb = keep.tile([P, J_PASSES, PACK], F32, name="cb_sb")
-        nc.scalar.dma_start(cw_sb[:], cw.rearrange("(g p t) -> p g t", g=J_PASSES, t=PACK))
-        nc.scalar.dma_start(cb_sb[:], cb.rearrange("(g p t) -> p g t", g=J_PASSES, t=PACK))
-
-        load_x(1)
-
-        plane1 = keep.tile([P, J], U8, name="plane1", align_bytes=64)
-        nc.vector.memset(plane1[:].bitcast(I32), 0)
-
-        cw_flat = cw_sb[:].rearrange("p g t -> p (g t)")
-        cb_flat = cb_sb[:].rearrange("p g t -> p (g t)")
-        sign = keep.tile([P, J_PASSES * PACK], F32, name="sign")
-        mag = keep.tile([P, J_PASSES * PACK], F32, name="mag")
-        root = keep.tile([P, J_PASSES * PACK], F32, name="root")
-        shift = keep.tile([P, J_PASSES * PACK], F32, name="shift")
-        nc.scalar.activation(sign[:], cw_flat, ACT.Sign)
-        nc.scalar.activation(mag[:], cw_flat, ACT.Abs)
-        nc.scalar.activation(root[:], mag[:], ACT.Sqrt, bias=SQRT_FLOOR)
-
-        scale_picked = keep.tile([P, J], U8, name="scale_picked", tag="scale_picked", align_bytes=64)
-        nc.vector.tensor_copy(scale_picked[:], scale_win[:].indirect(offsets[:]))
-        plane0 = keep.tile([P, J], U8, name="plane0", align_bytes=64)
-        nc.vector.tensor_copy(
-            out=plane0[:].rearrange("q (g t p) -> q g p t", g=J_PASSES, t=PACK),
-            in_=scale_picked[:].rearrange("q (g p t) -> q g p t", g=J_PASSES, t=PACK),
-        )
-        for q in range(1, QUADS):
-            nc.sync.dma_start(plane0[32 * q : 32 * q + 4, :].bitcast(I32), plane0[4 * q : 4 * q + 4, :].bitcast(I32))
-        for q in range(QUADS):
+        x_last = []
+        for h in range(2):
+            x_last.append(keep.tile([P, PACK, HALF], F32, name=f"x_last{h}", tag=f"x_last{h}", align_bytes=64))
             nc.sync.dma_start(
+                x_last[h][:],
+                x[PASS : 2 * PASS, h * HALF : (h + 1) * HALF].rearrange("(p t) m -> p t m", t=PACK),
+            )
+
+        ident = keep.tile([P, P], F32, name="ident")
+        make_identity(nc, ident[:])
+        plane1 = keep.tile([P, J], U8, name="plane1", align_bytes=64)
+        nc.gpsimd.memset(plane1[:].bitcast(I32), 0)
+
+        turned = psum.tile([P, PACK, P], F32, name="turned", tag="bank")
+        for t in range(PACK):
+            nc.tensor.transpose(turned[:, t, :], rows[:, t:PASS:PACK], ident[:])
+        cw_cols = turned[:, :, CW_ROW:CB_ROW]
+        cb_cols = turned[:, :, CB_ROW:P]
+        mag = keep.tile([P, PACK, J_PASSES], F32, name="mag")
+        root = keep.tile([P, PACK, J_PASSES], F32, name="root")
+        sign = keep.tile([P, J_PASSES, PACK], BF16, name="sign")
+        cb_sb = keep.tile([P, PACK, J_PASSES], F32, name="cb_sb")
+        shift = keep.tile([P, PACK, J_PASSES], F32, name="shift")
+        nc.scalar.activation(mag[:], cw_cols, ACT.Abs)
+        nc.scalar.activation(root[:], mag[:], ACT.Sqrt, bias=SQRT_FLOOR)
+        nc.scalar.activation(sign[:].rearrange("p g t -> p t g"), cw_cols, ACT.Sign)
+        nc.scalar.copy(cb_sb[:], cb_cols)
+        nc.gpsimd.tensor_tensor(shift[:], root[:], cb_sb[:], ALU.mult)
+
+        x_codes = [keep.tile([P, M], U32, name=f"x_codes{a}", align_bytes=64) for a in range(K_PASSES)]
+        x_planes = [keep.tile([P, M], U8, name=f"x_plane{a}", align_bytes=64) for a in range(K_PASSES)]
+        x_woven = [keep.tile([P, M, PACK], BF16, name="x_woven0", align_bytes=64)]
+
+        def quantize(codes, plane, woven):
+            nc.vector.quantize_mx(out=codes.bitcast(FP8X4), scales=plane, in_=woven.rearrange("p m t -> p (m t)"))
+
+        interleave(nc.scalar.copy, x_woven[0][:], x_first[:])
+        warm = keep.tile([P, 1], F32, name="warm")
+        nc.scalar.activation(warm[:], x_woven[0][:, M - 1, 0:1], ACT.Silu)
+
+        scale_picked = keep.tile([P, J], U8, name="scale_picked", tag="x_woven1", align_bytes=64)
+        nc.vector.tensor_copy(scale_picked[:], scale_win[:].indirect(offsets[:]))
+        plane0 = keep.tile([P, J], U8, name="plane0", tag="rows", align_bytes=64)
+        nc.vector.tensor_copy(
+            out=plane0[:].rearrange("q (g t p) -> q g t p", g=J_PASSES, t=PACK),
+            in_=scale_picked[:].rearrange("q (g p t) -> q g t p", g=J_PASSES, t=PACK),
+        )
+        quantize(x_codes[0][:], x_planes[0][:], x_woven[0][:])
+
+        for q in range(1, QUADS):
+            nc.scalar.dma_start(plane0[32 * q : 32 * q + 4, :].bitcast(I32), plane0[4 * q : 4 * q + 4, :].bitcast(I32))
+        for q in range(QUADS):
+            nc.scalar.dma_start(
                 plane1[32 * q : 32 * q + 4, :].bitcast(I32), plane0[16 + 4 * q : 20 + 4 * q, :].bitcast(I32)
             )
         planes = (plane0, plane1)
 
-        nc.vector.tensor_tensor(shift[:], root[:], cb_flat, ALU.mult)
+        x_woven.append(keep.tile([P, M, PACK], BF16, name="x_woven1", tag="x_woven1", align_bytes=64))
+        for h in range(2):
+            interleave(nc.scalar.copy, x_woven[1][:, h * HALF : (h + 1) * HALF, :], x_last[h][:])
 
-
-        centres = {}
-
-        def pick_words(g):
-            picked = keep.tile([P, PASS], U32, name="picked", align_bytes=64)
-            nc.vector.tensor_copy(picked[:], word_win[:].indirect(offsets[:, 32 * g : 32 * (g + 1)]))
-            return picked
-
-        def part_words(g, picked):
-            centres[g] = keep.tile([P, K_PASSES * PASS * 2], U8, name=f"centres{g}", tag="x_woven1" if g == 2 else f"centres{g}", align_bytes=64)
-            nc.vector.tensor_copy(
-                out=centres[g][:].bitcast(U16).rearrange("q (d t p) -> q d p t", d=K_PASSES, t=PACK),
-                in_=picked[:].bitcast(U16).rearrange("q (p t d) -> q d p t", d=K_PASSES, t=PACK),
-            )
-
-        x_codes = [keep.tile([P, M], U32, name=f"x_codes{a}", align_bytes=64) for a in range(K_PASSES)]
-        x_planes = [keep.tile([P, M], U8, name=f"x_plane{a}", align_bytes=64) for a in range(K_PASSES)]
-
-        def quantize_x(a):
-            woven = keep.tile([P, M, PACK], BF16, name=f"x_woven{a}", tag=f"x_woven{a}", align_bytes=64)
-            for h in range(2):
-                interleave(nc.scalar.copy, woven[:, h * X_HALF : (h + 1) * X_HALF, :], x_raw[a, h][:])
-            nc.vector.quantize_mx(
-                out=x_codes[a][:].bitcast(FP8X4),
-                scales=x_planes[a][:],
-                in_=woven[:].rearrange("p m t -> p (m t)"),
-            )
-
-        y_acc = [psum_y.tile([P, M], F32, name=f"y_acc{c}") for c in range(N_TILES)]
-
-        def first_stage(g):
-            h_rows = ring.tile([P, PACK, M], BF16, name="h_rows", align_bytes=64)
-            for t in range(PACK):
-                d_acc = psum_d.tile([P, M], F32, name="d_acc")
-                for a in range(K_PASSES):
-                    col = (a * PACK + t) * P
-                    nc.tensor.matmul_mx(
-                        out=d_acc[:],
-                        lhsT=centres[g][:, 2 * col : 2 * (col + P)].bitcast(FP4X4),
-                        lhsT_scale=planes[a][:, g * PASS + t * P : g * PASS + (t + 1) * P],
-                        rhs=x_codes[a][:].bitcast(FP8X4),
-                        rhs_scale=x_planes[a][:],
-                        start=(a == 0),
-                        stop=(a == K_PASSES - 1),
-                    )
-                u = g * PACK + t
-                nc.scalar.activation(
-                    h_rows[:, t, :], d_acc[:], ACT.Square, bias=shift[:, u : u + 1], scale=root[:, u : u + 1]
-                )
-                nc.vector.tensor_scalar(h_rows[:, t, :], h_rows[:, t, :], sign[:, u : u + 1], None, ALU.mult)
-            return h_rows
-
-        def second_stage(g, h_rows):
-            woven = ring.tile([P, M, PACK], BF16, name="h_woven", align_bytes=64)
-            interleave(nc.vector.tensor_copy, woven[:], h_rows[:])
-            h_codes = ring.tile([P, M], U32, name="h_codes", align_bytes=64)
-            h_plane = ring.tile([P, M], U8, name="h_plane", align_bytes=64)
-            nc.vector.quantize_mx(
-                out=h_codes[:].bitcast(FP8X4),
-                scales=h_plane[:],
-                in_=woven[:].rearrange("p m t -> p (m t)"),
-            )
-            for c in range(N_TILES):
-                nc.tensor.matmul_mx(
-                    out=y_acc[c][:],
-                    lhsT=al_codes[:, g, c * P : (c + 1) * P].bitcast(FP8X4),
-                    lhsT_scale=al_plane[4 * g :, c * P : (c + 1) * P],
-                    rhs=h_codes[:].bitcast(FP8X4),
-                    rhs_scale=h_plane[:],
-                    start=(g == 0),
-                    stop=(g == J_PASSES - 1),
-                )
-
-        quantize_x(0)
-        al_codes = keep.tile([P, J_PASSES, N], U32, name="al_codes", tag="x_woven0", align_bytes=64)
+        al_codes = keep.tile([P, J_PASSES, N], U32, name="al_codes", tag="x_last0", align_bytes=64)
         nc.sync.dma_start(
             al_codes[:].bitcast(I32),
             al_words.rearrange("g p n i -> p g (n i)").bitcast(I32),
         )
-        al_plane = keep.tile([P, N], U8, name="al_plane", tag="scale_picked", align_bytes=64)
+        al_plane = keep.tile([P, N], U8, name="al_plane", tag="x_last1", align_bytes=64)
         nc.gpsimd.memset(al_plane[:].bitcast(I32), 0)
         for q in range(QUADS):
             nc.sync.dma_start(
                 al_plane[32 * q : 32 * q + 16, :].bitcast(I32),
                 al_scales[:, 4 * q : 4 * q + 4, :].bitcast(I32),
             )
-        b_sb = keep.tile([P, N_TILES], F32, name="b_sb")
+
+        def pick_words(g, tag):
+            picked = keep.tile([P, PASS], U32, name=f"picked{g}", tag=tag, align_bytes=64)
+            nc.vector.tensor_copy(picked[:], word_win[:].indirect(offsets[:, 32 * g : 32 * (g + 1)]))
+            return picked
+
+        def part_words(centres, picked):
+            nc.vector.tensor_copy(
+                out=centres.bitcast(U16).rearrange("q (d t c i) -> q d c t i", d=K_PASSES, t=PACK, i=4),
+                in_=picked[:].bitcast(U16).rearrange("q (c i t d) -> q d c t i", d=K_PASSES, t=PACK, i=4),
+            )
+
+        width = K_PASSES * PASS * 2
+        picked0 = pick_words(0, "picked0")
+        centres0 = keep.tile([P, width], U8, name="centres0", tag="centres0", align_bytes=64)
+        part_words(centres0[:], picked0)
+        picked1 = pick_words(1, "picked1")
+        picked2 = pick_words(2, "picked2")
+        quantize(x_codes[1][:], x_planes[1][:], x_woven[1][:])
+        centres12 = keep.tile([P, 2 * width], U8, name="centres12", tag="x_woven1", align_bytes=64)
+        part_words(centres12[:, 0:width], picked1)
+        picked3 = pick_words(3, "picked1")
+        part_words(centres12[:, width : 2 * width], picked2)
+        centres3 = keep.tile([P, width], U8, name="centres3", align_bytes=64)
+        part_words(centres3[:], picked3)
+        centres = (centres0[:], centres12[:, 0:width], centres12[:, width : 2 * width], centres3[:])
+
+        def dot_products(g, t):
+            d_acc = psum.tile([P, M], F32, name="d_acc", tag="bank")
+            for a in range(K_PASSES):
+                col = (a * PACK + t) * P
+                nc.tensor.matmul_mx(
+                    out=d_acc[:],
+                    lhsT=centres[g][:, 2 * col : 2 * (col + P)].bitcast(FP4X4),
+                    lhsT_scale=planes[a][:, g * PASS + t * P : g * PASS + (t + 1) * P],
+                    rhs=x_codes[a][:].bitcast(FP8X4),
+                    rhs_scale=x_planes[a][:],
+                    start=(a == 0),
+                    stop=(a == K_PASSES - 1),
+                )
+            return d_acc
+
+        def square(dst, sums, g, t):
+            nc.scalar.activation(dst, sums, ACT.Square, bias=shift[:, t, g : g + 1], scale=root[:, t, g : g + 1])
+
+        def square_rows(g):
+            squares = keep.tile([P, PACK * M], BF16, name=f"squares{g}", tag=f"squares{g}", align_bytes=64)
+            for t in range(PACK):
+                square(squares[:, t * M : (t + 1) * M], dot_products(g, t)[:], g, t)
+            return squares
+
+        def square_pairs(g, banks, cols, name):
+            pairs = keep.tile([P, 2, cols.stop - cols.start, 2], BF16, name=name, align_bytes=64)
+            for t in range(PACK):
+                square(pairs[:, t // 2, :, t % 2], banks[t][:, cols], g, t)
+            return pairs
+
+        squares = [square_rows(0)]
+        b_sb = keep.tile([P, N_TILES], F32, name="b_sb", tag="centres0", align_bytes=64)
         with nc.allow_non_contiguous_dma(reason="one bias value a partition"):
             nc.sync.dma_start(b_sb[:], b.rearrange("(c p) -> p c", p=P))
+        squares.append(square_rows(1))
+        pairs2 = square_pairs(2, [dot_products(2, t) for t in range(PACK)], slice(0, M), "pairs2")
+        last_banks = [dot_products(LAST, t) for t in range(PACK)]
+        halves = [slice(h * HALF, (h + 1) * HALF) for h in range(2)]
+        last_pairs = [square_pairs(LAST, last_banks, halves[h], f"last_pairs{h}") for h in range(2)]
 
-        for g in range(J_PASSES):
-            if g == 2:
-                quantize_x(1)
-            part_words(g, pick_words(g))
-        rows = first_stage(0)
-        for g in range(J_PASSES):
-            nxt = first_stage(g + 1) if g + 1 < J_PASSES else None
-            second_stage(g, rows)
-            rows = nxt
+        y_acc = [psum.tile([P, N_TILES, HALF], F32, name=f"y_acc{h}", tag="bank") for h in range(2)]
 
-        for c in range(N_TILES):
-            result = keep.tile([P, M], F32, name=f"result{c}")
-            nc.scalar.activation(result[:], y_acc[c][:], ACT.Silu, bias=b_sb[:, c : c + 1])
-            nc.sync.dma_start(out[c * P : (c + 1) * P, :], result[:])
+        def accumulate(g, h, codes, plane):
+            for c in range(N_TILES):
+                nc.tensor.matmul_mx(
+                    out=y_acc[h][:, c, :],
+                    lhsT=al_codes[:, g, c * P : (c + 1) * P].bitcast(FP8X4),
+                    lhsT_scale=al_plane[4 * g :, c * P : (c + 1) * P],
+                    rhs=codes.bitcast(FP8X4),
+                    rhs_scale=plane,
+                    start=(g == 0 and c == 0),
+                    stop=(g == LAST and c == N_TILES - 1),
+                )
+
+        def apply_signs(g):
+            h_rows = ring.tile([P, PACK, M], BF16, name="h_rows", align_bytes=64)
+            for t in range(PACK):
+                nc.vector.tensor_scalar(
+                    h_rows[:, t, :], squares[g][:, t * M : (t + 1) * M], sign[:, g, t : t + 1], None, ALU.mult
+                )
+            return h_rows
+
+        def weave_rows(h_rows):
+            woven = ring.tile([P, M, PACK], BF16, name="h_woven", tag="h_woven", align_bytes=64)
+            interleave(nc.vector.tensor_copy, woven[:], h_rows[:])
+            return woven
+
+        def weave_pairs(g, pairs, cols):
+            woven = ring.tile([P, cols, PACK], BF16, name="h_woven", tag="h_woven", align_bytes=64)
+            signs = sign[:, g, :].rearrange("p (u e) -> p u e", e=2).unsqueeze(1).to_broadcast([P, cols, 2, 2])
+            nc.vector.tensor_tensor(
+                woven[:].rearrange("p m (u e) -> p m u e", e=2),
+                pairs[:].rearrange("p u m e -> p m u e"),
+                signs,
+                ALU.mult,
+            )
+            return woven
+
+        def quantize_h(woven, cols, name, tag):
+            h_codes = keep.tile([P, cols], U32, name=f"codes_{name}", tag=tag, align_bytes=64)
+            h_plane = keep.tile([P, cols], U8, name=f"plane_{name}", align_bytes=64)
+            quantize(h_codes[:], h_plane[:], woven[:])
+            return h_codes, h_plane
+
+        def second_stage(g, woven, tag):
+            h_codes, h_plane = quantize_h(woven, M, f"h{g}", tag)
+            for h in range(2):
+                accumulate(g, h, h_codes[:, halves[h]], h_plane[:, halves[h]])
+
+        woven0 = weave_rows(apply_signs(0))
+        h_rows1 = apply_signs(1)
+        second_stage(0, woven0, "squares1")
+        second_stage(1, weave_rows(h_rows1), "codes_h1")
+        second_stage(2, weave_pairs(2, pairs2, M), "codes_h2")
+        for h in range(2):
+            h_codes, h_plane = quantize_h(weave_pairs(LAST, last_pairs[h], HALF), HALF, f"last{h}", f"codes_last{h}")
+            accumulate(LAST, h, h_codes[:], h_plane[:])
+            for c in range(N_TILES):
+                result = keep.tile([P, HALF], F32, name=f"result{h}{c}")
+                nc.scalar.activation(result[:], y_acc[h][:, c, :], ACT.Silu, bias=b_sb[:, c : c + 1])
+                nc.sync.dma_start(out[c * P : (c + 1) * P, halves[h]], result[:])

from contextlib import ExitStack

import concourse.mybir as mybir
from concourse.masks import make_identity

K, M, N, J, T = 1024, 512, 256, 2048, 4096
FLOPS = 2 * K * M * J + 2 * J * M * N

F32 = mybir.dt.float32
BF16 = mybir.dt.bfloat16
I32 = mybir.dt.int32
U32 = mybir.dt.uint32
U16 = mybir.dt.uint16
U8 = mybir.dt.uint8
FP8X4 = mybir.dt.float8_e4m3fn_x4
FP4X4 = mybir.dt.float4_e2m1fn_x4
ACT = mybir.ActivationFunctionType
ALU = mybir.AluOpType

P = 128
PACK = 4
PASS = P * PACK
K_PASSES = K // PASS
J_PASSES = J // PASS
N_TILES = N // P
QUADS = 4
HALF = M // 2
CW_ROW = P - 2 * J_PASSES
CB_ROW = P - J_PASSES
SQRT_FLOOR = 2.0 ** -116
LAST = J_PASSES - 1


def interleave(copy, dst, src):
    copy(
        out=dst.rearrange("p (c i) t -> p c t i", i=PACK),
        in_=src.rearrange("p t (c i) -> p c t i", i=PACK),
    )


def tile_list_kernl_poly2_silu_kernel(
    tc, x, tab_words, tab_scales, cw, cb, al_words, al_scales, b, offs, out
):
    nc = tc.nc
    with ExitStack() as ctx:
        keep = ctx.enter_context(tc.tile_pool(name="keep", bufs=1))
        ring = ctx.enter_context(tc.tile_pool(name="ring", bufs=2))
        psum = ctx.enter_context(tc.psum_pool(name="psum", bufs=8))

        offsets = keep.tile([P, J // 16], U16, name="offsets")
        nc.sync.dma_start(offsets[:], offs)

        scale_win = keep.tile([P, T], U8, name="scale_win", align_bytes=64)
        nc.sync.dma_start(
            scale_win[0:32, :].bitcast(I32),
            tab_scales.rearrange("a q t -> (a q) t").bitcast(I32),
        )
        nc.vector.memset(scale_win[32:64, :].bitcast(I32), 0)
        nc.vector.memset(scale_win[64:128, :].bitcast(I32), 0)

        rows = keep.tile([P, PASS], F32, name="rows", tag="rows", align_bytes=64)
        nc.gpsimd.memset(rows[0:CW_ROW, :], 0.0)
        nc.sync.dma_start(rows[CW_ROW:CB_ROW, :], cw.rearrange("(g j) -> g j", g=J_PASSES))
        nc.sync.dma_start(rows[CB_ROW:P, :], cb.rearrange("(g j) -> g j", g=J_PASSES))

        x_first = keep.tile([P, PACK, M], F32, name="x_first", tag="x_first", align_bytes=64)
        nc.sync.dma_start(x_first[:], x[0:PASS, :].rearrange("(p t) m -> p t m", t=PACK))

        word_win = keep.tile([P, T], U32, name="word_win", align_bytes=64)
        nc.sync.dma_start(
            word_win[:].bitcast(I32),
            tab_words[0].rearrange("p t i -> p (t i)").bitcast(I32),
        )

        x_last = []
        for h in range(2):
            x_last.append(keep.tile([P, PACK, HALF], F32, name=f"x_last{h}", tag=f"x_last{h}", align_bytes=64))
            nc.sync.dma_start(
                x_last[h][:],
                x[PASS : 2 * PASS, h * HALF : (h + 1) * HALF].rearrange("(p t) m -> p t m", t=PACK),
            )

        ident = keep.tile([P, P], F32, name="ident")
        make_identity(nc, ident[:])
        plane1 = keep.tile([P, J], U8, name="plane1", align_bytes=64)
        nc.gpsimd.memset(plane1[:].bitcast(I32), 0)

        turned = psum.tile([P, PACK, P], F32, name="turned", tag="bank")
        for t in range(PACK):
            nc.tensor.transpose(turned[:, t, :], rows[:, t:PASS:PACK], ident[:])
        cw_cols = turned[:, :, CW_ROW:CB_ROW]
        cb_cols = turned[:, :, CB_ROW:P]
        mag = keep.tile([P, PACK, J_PASSES], F32, name="mag")
        root = keep.tile([P, PACK, J_PASSES], F32, name="root")
        sign = keep.tile([P, J_PASSES, PACK], BF16, name="sign")
        cb_sb = keep.tile([P, PACK, J_PASSES], F32, name="cb_sb")
        shift = keep.tile([P, PACK, J_PASSES], F32, name="shift")
        nc.scalar.activation(mag[:], cw_cols, ACT.Abs)
        nc.scalar.activation(root[:], mag[:], ACT.Sqrt, bias=SQRT_FLOOR)
        nc.scalar.activation(sign[:].rearrange("p g t -> p t g"), cw_cols, ACT.Sign)
        nc.scalar.copy(cb_sb[:], cb_cols)
        nc.gpsimd.tensor_tensor(shift[:], root[:], cb_sb[:], ALU.mult)

        x_codes = [keep.tile([P, M], U32, name=f"x_codes{a}", align_bytes=64) for a in range(K_PASSES)]
        x_planes = [keep.tile([P, M], U8, name=f"x_plane{a}", align_bytes=64) for a in range(K_PASSES)]
        x_woven = [keep.tile([P, M, PACK], BF16, name="x_woven0", align_bytes=64)]

        def quantize(codes, plane, woven):
            nc.vector.quantize_mx(out=codes.bitcast(FP8X4), scales=plane, in_=woven.rearrange("p m t -> p (m t)"))

        interleave(nc.scalar.copy, x_woven[0][:], x_first[:])
        warm = keep.tile([P, 1], F32, name="warm")
        nc.scalar.activation(warm[:], x_woven[0][:, M - 1, 0:1], ACT.Silu)

        scale_picked = keep.tile([P, J], U8, name="scale_picked", tag="x_woven1", align_bytes=64)
        nc.vector.tensor_copy(scale_picked[:], scale_win[:].indirect(offsets[:]))
        plane0 = keep.tile([P, J], U8, name="plane0", tag="rows", align_bytes=64)
        nc.vector.tensor_copy(
            out=plane0[:].rearrange("q (g t p) -> q g t p", g=J_PASSES, t=PACK),
            in_=scale_picked[:].rearrange("q (g p t) -> q g t p", g=J_PASSES, t=PACK),
        )
        quantize(x_codes[0][:], x_planes[0][:], x_woven[0][:])

        for q in range(1, QUADS):
            nc.scalar.dma_start(plane0[32 * q : 32 * q + 4, :].bitcast(I32), plane0[4 * q : 4 * q + 4, :].bitcast(I32))
        for q in range(QUADS):
            nc.scalar.dma_start(
                plane1[32 * q : 32 * q + 4, :].bitcast(I32), plane0[16 + 4 * q : 20 + 4 * q, :].bitcast(I32)
            )
        planes = (plane0, plane1)

        x_woven.append(keep.tile([P, M, PACK], BF16, name="x_woven1", tag="x_woven1", align_bytes=64))
        for h in range(2):
            interleave(nc.scalar.copy, x_woven[1][:, h * HALF : (h + 1) * HALF, :], x_last[h][:])

        al_codes = keep.tile([P, J_PASSES, N], U32, name="al_codes", tag="x_last0", align_bytes=64)
        nc.sync.dma_start(
            al_codes[:].bitcast(I32),
            al_words.rearrange("g p n i -> p g (n i)").bitcast(I32),
        )
        al_plane = keep.tile([P, N], U8, name="al_plane", tag="x_last1", align_bytes=64)
        nc.gpsimd.memset(al_plane[:].bitcast(I32), 0)
        for q in range(QUADS):
            nc.sync.dma_start(
                al_plane[32 * q : 32 * q + 16, :].bitcast(I32),
                al_scales[:, 4 * q : 4 * q + 4, :].bitcast(I32),
            )

        def pick_words(g, tag):
            picked = keep.tile([P, PASS], U32, name=f"picked{g}", tag=tag, align_bytes=64)
            nc.vector.tensor_copy(picked[:], word_win[:].indirect(offsets[:, 32 * g : 32 * (g + 1)]))
            return picked

        def part_words(centres, picked):
            nc.vector.tensor_copy(
                out=centres.bitcast(U16).rearrange("q (d t c i) -> q d c t i", d=K_PASSES, t=PACK, i=4),
                in_=picked[:].bitcast(U16).rearrange("q (c i t d) -> q d c t i", d=K_PASSES, t=PACK, i=4),
            )

        width = K_PASSES * PASS * 2
        picked0 = pick_words(0, "picked0")
        centres0 = keep.tile([P, width], U8, name="centres0", tag="centres0", align_bytes=64)
        part_words(centres0[:], picked0)
        picked1 = pick_words(1, "picked1")
        picked2 = pick_words(2, "picked2")
        quantize(x_codes[1][:], x_planes[1][:], x_woven[1][:])
        centres12 = keep.tile([P, 2 * width], U8, name="centres12", tag="x_woven1", align_bytes=64)
        part_words(centres12[:, 0:width], picked1)
        picked3 = pick_words(3, "picked1")
        part_words(centres12[:, width : 2 * width], picked2)
        centres3 = keep.tile([P, width], U8, name="centres3", align_bytes=64)
        part_words(centres3[:], picked3)
        centres = (centres0[:], centres12[:, 0:width], centres12[:, width : 2 * width], centres3[:])

        def dot_products(g, t):
            d_acc = psum.tile([P, M], F32, name="d_acc", tag="bank")
            for a in range(K_PASSES):
                col = (a * PACK + t) * P
                nc.tensor.matmul_mx(
                    out=d_acc[:],
                    lhsT=centres[g][:, 2 * col : 2 * (col + P)].bitcast(FP4X4),
                    lhsT_scale=planes[a][:, g * PASS + t * P : g * PASS + (t + 1) * P],
                    rhs=x_codes[a][:].bitcast(FP8X4),
                    rhs_scale=x_planes[a][:],
                    start=(a == 0),
                    stop=(a == K_PASSES - 1),
                )
            return d_acc

        def square(dst, sums, g, t):
            nc.scalar.activation(dst, sums, ACT.Square, bias=shift[:, t, g : g + 1], scale=root[:, t, g : g + 1])

        def square_rows(g):
            squares = keep.tile([P, PACK * M], BF16, name=f"squares{g}", tag=f"squares{g}", align_bytes=64)
            for t in range(PACK):
                square(squares[:, t * M : (t + 1) * M], dot_products(g, t)[:], g, t)
            return squares

        def square_pairs(g, banks, cols, name):
            pairs = keep.tile([P, 2, cols.stop - cols.start, 2], BF16, name=name, align_bytes=64)
            for t in range(PACK):
                square(pairs[:, t // 2, :, t % 2], banks[t][:, cols], g, t)
            return pairs

        squares = [square_rows(0)]
        b_sb = keep.tile([P, N_TILES], F32, name="b_sb", tag="centres0", align_bytes=64)
        with nc.allow_non_contiguous_dma(reason="one bias value a partition"):
            nc.sync.dma_start(b_sb[:], b.rearrange("(c p) -> p c", p=P))
        squares.append(square_rows(1))
        pairs2 = square_pairs(2, [dot_products(2, t) for t in range(PACK)], slice(0, M), "pairs2")
        last_banks = [dot_products(LAST, t) for t in range(PACK)]
        halves = [slice(h * HALF, (h + 1) * HALF) for h in range(2)]
        last_pairs = [square_pairs(LAST, last_banks, halves[h], f"last_pairs{h}") for h in range(2)]

        y_acc = [psum.tile([P, N_TILES, HALF], F32, name=f"y_acc{h}", tag="bank") for h in range(2)]

        def accumulate(g, h, codes, plane):
            for c in range(N_TILES):
                nc.tensor.matmul_mx(
                    out=y_acc[h][:, c, :],
                    lhsT=al_codes[:, g, c * P : (c + 1) * P].bitcast(FP8X4),
                    lhsT_scale=al_plane[4 * g :, c * P : (c + 1) * P],
                    rhs=codes.bitcast(FP8X4),
                    rhs_scale=plane,
                    start=(g == 0 and c == 0),
                    stop=(g == LAST and c == N_TILES - 1),
                )

        def apply_signs(g):
            h_rows = ring.tile([P, PACK, M], BF16, name="h_rows", align_bytes=64)
            for t in range(PACK):
                nc.vector.tensor_scalar(
                    h_rows[:, t, :], squares[g][:, t * M : (t + 1) * M], sign[:, g, t : t + 1], None, ALU.mult
                )
            return h_rows

        def weave_rows(h_rows):
            woven = ring.tile([P, M, PACK], BF16, name="h_woven", tag="h_woven", align_bytes=64)
            interleave(nc.vector.tensor_copy, woven[:], h_rows[:])
            return woven

        def weave_pairs(g, pairs, cols):
            woven = ring.tile([P, cols, PACK], BF16, name="h_woven", tag="h_woven", align_bytes=64)
            signs = sign[:, g, :].rearrange("p (u e) -> p u e", e=2).unsqueeze(1).to_broadcast([P, cols, 2, 2])
            nc.vector.tensor_tensor(
                woven[:].rearrange("p m (u e) -> p m u e", e=2),
                pairs[:].rearrange("p u m e -> p m u e"),
                signs,
                ALU.mult,
            )
            return woven

        def quantize_h(woven, cols, name, tag):
            h_codes = keep.tile([P, cols], U32, name=f"codes_{name}", tag=tag, align_bytes=64)
            h_plane = keep.tile([P, cols], U8, name=f"plane_{name}", align_bytes=64)
            quantize(h_codes[:], h_plane[:], woven[:])
            return h_codes, h_plane

        def second_stage(g, woven, tag):
            h_codes, h_plane = quantize_h(woven, M, f"h{g}", tag)
            for h in range(2):
                accumulate(g, h, h_codes[:, halves[h]], h_plane[:, halves[h]])

        woven0 = weave_rows(apply_signs(0))
        h_rows1 = apply_signs(1)
        second_stage(0, woven0, "squares1")
        second_stage(1, weave_rows(h_rows1), "codes_h1")
        second_stage(2, weave_pairs(2, pairs2, M), "codes_h2")
        for h in range(2):
            h_codes, h_plane = quantize_h(weave_pairs(LAST, last_pairs[h], HALF), HALF, f"last{h}", f"codes_last{h}")
            accumulate(LAST, h, h_codes[:], h_plane[:])
            for c in range(N_TILES):
                result = keep.tile([P, HALF], F32, name=f"result{h}{c}")
                nc.scalar.activation(result[:], y_acc[h][:, c, :], ACT.Silu, bias=b_sb[:, c : c + 1])
                nc.sync.dma_start(out[c * P : (c + 1) * P, halves[h]], result[:])
